import numpy as np
import ml_dtypes


def mxq(x, axis, fmt="e4m3"):
    dtype, down = {"e4m3": (ml_dtypes.float8_e4m3fn, 7), "e5m2": (ml_dtypes.float8_e5m2, 14)}[fmt]
    v = np.moveaxis(np.asarray(x, np.float32).astype(ml_dtypes.bfloat16).astype(np.float64), axis, -1)
    blocks = v.reshape(v.shape[:-1] + (-1, 32))
    amax = np.abs(blocks).max(-1, keepdims=True)
    byte = np.maximum(np.where(amax > 0, np.frexp(amax)[1] - 1 + 127, 0) - down, 1)
    scale = np.exp2(byte - 127.0)
    codes = (blocks / scale).astype(np.float32).astype(dtype).astype(np.float64)
    return np.moveaxis((codes * scale).reshape(v.shape), -1, axis)


WIDE = False


def mx_kscale(k):
    if not WIDE:
        return np.ones(k)
    levels = np.array([10, -10, 5, -5, 0])
    if k % 512:
        return np.exp2(np.random.permutation(np.resize(levels, k // 32))).repeat(32)
    a = np.empty((k // 512, 16))
    for p in range(k // 512):
        a[p, :8] = np.random.permutation(np.resize(levels, 8))
        for g in range(8):
            far = levels[np.abs(levels - a[p, g]) >= 10]
            a[p, g + 8] = far[np.random.randint(len(far))]
    return np.exp2(a.ravel()).repeat(32)


def f64(x):
    return np.asarray(x).astype(np.float64)


def striped(idx):
    return np.tile(np.asarray(idx).reshape(-1, 16).T, (8, 1)).astype(np.uint16)


def unstriped(offs):
    return offs[:16].T.reshape(-1).astype(np.int64)


E2M1 = np.array([0.0, 0.5, 1.0, 1.5, 2.0, 3.0, 4.0, 6.0, -0.0, -0.5, -1.0, -1.5, -2.0, -3.0, -4.0, -6.0])


def pack_weight(w, fmt):
    k, n = w.shape
    w = f64(np.asarray(w, np.float32).astype(ml_dtypes.bfloat16)).reshape(k // 32, 32, n)
    amax = np.abs(w).max(1)
    if fmt == "e4m3":
        byte = np.frexp(amax)[1] - 1 + 127 - 7
    else:
        mant, ex = np.frexp(amax / 6.0)
        byte = np.where(mant > 0.5, ex, ex - 1) + 127
    byte = np.clip(np.where(amax > 0, byte, 1), 1, 254)
    scaled = (w * np.exp2(127.0 - byte)[:, None, :]).reshape(k, n).astype(np.float32)
    by_word = np.ascontiguousarray(scaled.reshape(k // 512, 128, 4, n).transpose(0, 1, 3, 2))
    if fmt == "e4m3":
        words = by_word.astype(ml_dtypes.float8_e4m3fn).view(np.uint8)
    else:
        c = by_word.astype(ml_dtypes.float4_e2m1fn).view(np.uint8) & 0xF
        words = (c[..., 0::2] | (c[..., 1::2] << 4)).reshape(k // 512, 128, 2 * n)
    return np.ascontiguousarray(words), np.ascontiguousarray(byte.astype(np.uint8).reshape(k // 512, 16, n))


def unpack_weight(words, scales, fmt):
    g, _, n = scales.shape
    words = np.ascontiguousarray(words).reshape(g, 128, n, -1)
    if fmt == "e4m3":
        vals = words.view(ml_dtypes.float8_e4m3fn).astype(np.float64)
    else:
        nib = np.empty((g, 128, n, 4), np.uint8)
        nib[..., 0::2] = words & 0xF
        nib[..., 1::2] = words >> 4
        vals = E2M1[nib]
    vals = vals * np.repeat(np.exp2(scales.astype(np.float64) - 127.0), 8, axis=1)[..., None]
    return vals.transpose(0, 1, 3, 2).reshape(g * 512, n)


D, E, T, I, Q, G = 512, 512, 2048, 512, 128, 64


def setup_inputs():
    n = np.random.standard_normal
    idx = np.random.permutation(T)[:I]
    fd = mx_kscale(D)
    fe = mx_kscale(E)
    keysp = pack_weight(n((D, T)) / fd[:, None], "e4m3")
    valsp = pack_weight(n((E, T)) / fe[:, None], "e4m3")
    return {
        "query": (n((D, Q)) * 0.8 / np.sqrt(D) * fd[:, None]).astype(np.float32),
        "keys_words": keysp[0],
        "keys_scales": keysp[1],
        "mix": (np.random.uniform(0.2, 0.8, (Q, 1))).astype(np.float32),
        "gout": (n((E, Q)) * 1 / np.sqrt(E) * fe[:, None]).astype(np.float32),
        "vals_words": valsp[0],
        "vals_scales": valsp[1],
        "base": (0.5 * n((Q, I))).astype(np.float32),
        "offs": striped(idx),
    }


def reference(query, keys_words, keys_scales, mix, gout, vals_words, vals_scales, base, offs):
    idx = unstriped(offs)
    keysu = unpack_weight(keys_words, keys_scales, "e4m3")
    valsu = unpack_weight(vals_words, vals_scales, "e4m3")
    queryq = mxq(f64(query), 0, "e4m3")
    keysidxg = keysu[:, idx]
    a = queryq.T @ keysidxg
    p = np.exp(a - np.max(a, axis=1, keepdims=True))
    goutq = mxq(f64(gout), 0, "e4m3")
    valsidxg = valsu[:, idx]
    c0 = goutq.T @ valsidxg
    dpr = c0 * f64(mix)
    dpm = dpr.reshape(Q, G, I // G).sum(axis=2)
    e1 = dpm / 8.0
    r1 = np.repeat(e1, I // G, axis=1)
    dr = c0 * (1.0 - f64(mix)) + r1
    dp = dr / np.sum(p, axis=1, keepdims=True) + np.sum(dr * p / np.square(np.sum(p, axis=1, keepdims=True)) * (-1.0), axis=1, keepdims=True)
    da = dp * p
    hda = da * 512.0 * 2.0 * 512.0
    hdp = hda * p
    hp = hda * dp + np.sum(hdp * dr / np.square(np.sum(p, axis=1, keepdims=True)) * (-1.0), axis=1, keepdims=True) + np.sum(hdp, axis=1, keepdims=True) * (-1.0) / np.square(np.sum(p, axis=1, keepdims=True)) * dr + np.sum(np.sum(hdp, axis=1, keepdims=True) * (-1.0) * dr * p / np.square(np.square(np.sum(p, axis=1, keepdims=True))) * (-1.0), axis=1, keepdims=True) * np.sum(p, axis=1, keepdims=True) * 2.0
    ha = hp * p
    y = ha + f64(base)
    return y

@@ -1,0 +1,216 @@
+import math
+from contextlib import ExitStack
+
+import concourse.mybir as mybir
+
+F32 = mybir.dt.float32
+BF16 = mybir.dt.bfloat16
+I32 = mybir.dt.int32
+U32 = mybir.dt.uint32
+U16 = mybir.dt.uint16
+U8 = mybir.dt.uint8
+FP8X4 = mybir.dt.float8_e4m3fn_x4
+ALU = mybir.AluOpType
+ACT = mybir.ActivationFunctionType
+AXIS_X = mybir.AxisListType.X
+
+P = 128
+PACK = 4
+TOKENS = 2048
+SLOTS = 512
+ROWS = 128
+RUN = 8
+HALF = SLOTS // 2
+QUADRANT = 32
+VALS_PLANE = 4
+ROOT_K = math.sqrt(512.0 * 2.0 * 512.0)
+
+FLOPS = 2 * 2 * 512 * ROWS * SLOTS
+
+
+def tile_attend_gpdirect_smoothpage_kernel(
+    tc, query, keys_words, keys_scales, mix, gout, vals_words, vals_scales, base, offs, out
+):
+    nc = tc.nc
+    halves = [slice(0, HALF), slice(HALF, SLOTS)]
+
+    with ExitStack() as ctx:
+        sb = ctx.enter_context(tc.tile_pool(name="sb", bufs=1))
+        psum = ctx.enter_context(tc.psum_pool(name="psum", bufs=1))
+
+        offsets = sb.tile([P, SLOTS // 16], U16, name="offsets")
+        key_byte_pool = sb.tile([P, TOKENS], U8, name="key_byte_pool", align_bytes=64)
+        val_byte_pool = sb.tile([P, TOKENS], U8, name="val_byte_pool", align_bytes=64)
+        key_word_pool = sb.tile([P, TOKENS], U32, name="key_word_pool", align_bytes=64)
+        val_word_pool = sb.tile([P, TOKENS], U32, name="val_word_pool", align_bytes=64)
+        query_raw = sb.tile([P, PACK, ROWS], F32, name="query_raw")
+        gout_raw = sb.tile([P, PACK, ROWS], F32, name="gout_raw")
+        base_sb = sb.tile([P, SLOTS], F32, name="base_sb")
+        mix_sb = sb.tile([P, 1], F32, name="mix_sb")
+
+        nc.vector.memset(key_byte_pool[:].bitcast(I32), 0)
+        nc.vector.memset(val_byte_pool[:].bitcast(I32), 0)
+
+        def load_scale_rows(queue, byte_pool, scales, plane, r):
+            queue.dma_start(
+                out=byte_pool[plane + r : P : QUADRANT, :].bitcast(I32),
+                in_=scales[0, r:16:4, :].bitcast(I32),
+            )
+
+        nc.sync.dma_start(offsets[:], offs)
+        for r in range(4):
+            load_scale_rows(nc.scalar, key_byte_pool, keys_scales, 0, r)
+        nc.sync.dma_start(out=query_raw[:], in_=query.rearrange("(p j) q -> p j q", j=PACK))
+        nc.sync.dma_start(out=gout_raw[:], in_=gout.rearrange("(p j) q -> p j q", j=PACK))
+        for r in range(4):
+            load_scale_rows(nc.scalar if r < 2 else nc.gpsimd, val_byte_pool, vals_scales, VALS_PLANE, r)
+        nc.sync.dma_start(
+            out=key_word_pool[:].bitcast(I32),
+            in_=keys_words[0].rearrange("p n t -> p (n t)").bitcast(I32),
+        )
+        nc.sync.dma_start(
+            out=val_word_pool[:].bitcast(I32),
+            in_=vals_words[0].rearrange("p n t -> p (n t)").bitcast(I32),
+        )
+        nc.gpsimd.dma_start(out=mix_sb[:], in_=mix)
+        nc.sync.dma_start(out=base_sb[:], in_=base)
+
+        keep = sb.tile([P, 1], F32, name="keep")
+        share = sb.tile([P, 1], F32, name="share")
+        nc.gpsimd.tensor_scalar(keep[:], mix_sb[:], -1.0, 1.0, ALU.mult, ALU.add)
+        nc.gpsimd.tensor_scalar(share[:], mix_sb[:], 1.0 / RUN, 0.0, ALU.mult, ALU.add)
+
+        key_bytes = sb.tile([P, SLOTS], U8, name="key_bytes", align_bytes=64)
+        val_bytes = sb.tile([P, SLOTS], U8, name="val_bytes", align_bytes=64)
+        nc.vector.tensor_copy(key_bytes[:], key_byte_pool[:].indirect(offsets[:]))
+        nc.vector.tensor_copy(val_bytes[:], val_byte_pool[:].indirect(offsets[:]))
+
+        grouped = sb.tile([P, 2, ROWS, PACK], BF16, name="grouped", align_bytes=64)
+        nc.scalar.copy(out=grouped[:, 0], in_=query_raw[:].rearrange("p j q -> p q j"))
+        nc.scalar.copy(out=grouped[:, 1], in_=gout_raw[:].rearrange("p j q -> p q j"))
+        row_codes = sb.tile([P, 2 * ROWS], U32, name="row_codes", align_bytes=64)
+        row_scales = sb.tile([P, 2 * ROWS], U8, name="row_scales", align_bytes=64)
+        nc.vector.quantize_mx(
+            out=row_codes[:].bitcast(FP8X4),
+            scales=row_scales[:],
+            in_=grouped[:].rearrange("p s q j -> p (s q j)"),
+        )
+
+        key_words = sb.tile([P, SLOTS], U32, name="key_words", align_bytes=64)
+        nc.vector.tensor_copy(key_words[:], key_word_pool[:].indirect(offsets[:]))
+        scores = psum.tile([P, SLOTS], F32, name="scores")
+        nc.tensor.matmul_mx(
+            out=scores[:],
+            lhsT=row_codes[:, 0:ROWS].bitcast(FP8X4),
+            lhsT_scale=row_scales[:, 0:ROWS],
+            rhs=key_words[:].bitcast(FP8X4),
+            rhs_scale=key_bytes[:],
+            start=True,
+            stop=True,
+        )
+
+        neg_max = sb.tile([P, 1], F32, name="neg_max")
+        nc.vector.tensor_reduce(neg_max[:], scores[:], AXIS_X, ALU.max, negate=True)
+        p = sb.tile([P, SLOTS], F32, name="p")
+        p_sum = sb.tile([P, 1], F32, name="p_sum")
+        nc.scalar.activation(p[:], scores[:], ACT.Exp, bias=neg_max[:], scale=1.0, accum_out=p_sum[:])
+        inv_sum = sb.tile([P, 1], F32, name="inv_sum")
+        nc.vector.reciprocal(inv_sum[:], p_sum[:])
+        r_sq = sb.tile([P, SLOTS], F32, name="r_sq")
+        r_sq_sum = sb.tile([P, 1], F32, name="r_sq_sum")
+        nc.scalar.activation(r_sq[:], p[:], ACT.Square, scale=inv_sum[:], accum_out=r_sq_sum[:])
+        r = sb.tile([P, SLOTS], F32, name="r")
+        nc.scalar.activation(r[:], p[:], ACT.Copy, scale=inv_sum[:])
+        r_sq_half = sb.tile([P, 1], F32, name="r_sq_half")
+        nc.scalar.activation(r_sq_half[:], r_sq_sum[:], ACT.Copy, scale=ROOT_K / 2.0)
+
+        val_words = [sb.tile([P, HALF], U32, name="val_words%d" % h, align_bytes=64) for h in range(2)]
+        c0 = [psum.tile([P, HALF], F32, name="c0_%d" % h) for h in range(2)]
+        for h in range(2):
+            list_cols = slice(h * HALF // 16, (h + 1) * HALF // 16)
+            nc.vector.tensor_copy(val_words[h][:], val_word_pool[:].indirect(offsets[:, list_cols]))
+            nc.tensor.matmul_mx(
+                out=c0[h][:],
+                lhsT=row_codes[:, ROWS : 2 * ROWS].bitcast(FP8X4),
+                lhsT_scale=row_scales[:, ROWS : 2 * ROWS],
+                rhs=val_words[h][:].bitcast(FP8X4),
+                rhs_scale=val_bytes[VALS_PLANE:P, halves[h]],
+                start=True,
+                stop=True,
+            )
+
+        runs = HALF // RUN
+        run_sum = [sb.tile([P, runs], F32, name="run_sum%d" % h) for h in range(2)]
+        run_mix = [sb.tile([P, runs], F32, name="run_mix%d" % h) for h in range(2)]
+        dr = sb.tile([P, SLOTS], F32, name="dr")
+        for h in range(2):
+            nc.vector.tensor_reduce(
+                run_sum[h][:], c0[h][:].rearrange("p (g j) -> p g j", j=RUN), AXIS_X, ALU.add
+            )
+        for h in range(2):
+            nc.vector.tensor_scalar(run_mix[h][:], run_sum[h][:], share[:], None, ALU.mult)
+        for h in range(2):
+            nc.vector.scalar_tensor_tensor(
+                dr[:, halves[h]].rearrange("p (g j) -> p g j", j=RUN),
+                c0[h][:].rearrange("p (g j) -> p g j", j=RUN),
+                keep[:],
+                run_mix[h][:].unsqueeze(2).to_broadcast([P, runs, RUN]),
+                ALU.mult,
+                ALU.add,
+            )
+
+        terms = sb.tile([P, SLOTS], F32, name="terms")
+        terms2 = sb.tile([P, SLOTS], F32, name="terms2")
+        mu = sb.tile([P, 1], F32, name="mu")
+        nc.vector.scalar_tensor_tensor(terms[:], dr[:], inv_sum[:], p[:], ALU.mult, ALU.mult, accum_out=mu[:])
+        raw_t1 = sb.tile([P, 1], F32, name="raw_t1")
+        nc.vector.scalar_tensor_tensor(
+            terms2[:], dr[:], ROOT_K / 2.0, r_sq[:], ALU.mult, ALU.mult, accum_out=raw_t1[:]
+        )
+
+        da = sb.tile([P, SLOTS], F32, name="da")
+        shift = sb.tile([P, 1], F32, name="shift")
+        shift_sq = sb.tile([P, 1], F32, name="shift_sq")
+        shift_sq_all = sb.tile([P, 1], F32, name="shift_sq_all")
+        square = sb.tile([P, SLOTS], F32, name="square")
+        square_sum = [sb.tile([P, 1], F32, name="square_sum%d" % h) for h in range(2)]
+
+        def make_da(h):
+            nc.vector.scalar_tensor_tensor(
+                da[:, halves[h]], dr[:, halves[h]], mu[:], r[:, halves[h]], ALU.subtract, ALU.mult
+            )
+
+        def make_square(h):
+            nc.scalar.activation(
+                square[:, halves[h]], da[:, halves[h]], ACT.Square,
+                bias=shift[:], scale=ROOT_K, accum_out=square_sum[h][:],
+            )
+
+        make_da(0)
+        nc.vector.scalar_tensor_tensor(shift[:], mu[:], r_sq_half[:], raw_t1[:], ALU.mult, ALU.subtract)
+        make_da(1)
+        make_square(0)
+        make_square(1)
+        nc.vector.tensor_tensor(shift_sq[:], shift[:], shift[:], ALU.mult)
+        nc.vector.scalar_tensor_tensor(shift_sq_all[:], shift[:], float(SLOTS), shift[:], ALU.mult, ALU.mult)
+
+        partial = sb.tile([P, SLOTS], F32, name="partial")
+        result = sb.tile([P, SLOTS], F32, name="result")
+        neg_t2 = sb.tile([P, 1], F32, name="neg_t2")
+
+        def make_partial(h):
+            nc.vector.scalar_tensor_tensor(
+                partial[:, halves[h]], square[:, halves[h]], shift_sq[:], base_sb[:, halves[h]],
+                ALU.subtract, ALU.add,
+            )
+
+        make_partial(0)
+        nc.vector.tensor_scalar(
+            neg_t2[:], shift_sq_all[:], square_sum[0][:], square_sum[1][:], ALU.subtract, ALU.subtract
+        )
+        make_partial(1)
+        for h in range(2):
+            nc.vector.scalar_tensor_tensor(
+                result[:, halves[h]], r[:, halves[h]], neg_t2[:], partial[:, halves[h]], ALU.mult, ALU.add
+            )
+            nc.sync.dma_start(out=out[:, halves[h]], in_=result[:, halves[h]])

@@ -40,9 +40,9 @@ def tile_attend_gpdirect_smoothpage_kernel(
 
         offsets = sb.tile([P, SLOTS // 16], U16, name="offsets")
         key_byte_pool = sb.tile([P, TOKENS], U8, name="key_byte_pool", align_bytes=64)
-        val_byte_pool = sb.tile([P, TOKENS], U8, name="val_byte_pool", align_bytes=64)
+        val_byte_pool = sb.tile([P, TOKENS], U8, name="val_byte_pool", tag="val_byte_pool", align_bytes=64)
         key_word_pool = sb.tile([P, TOKENS], U32, name="key_word_pool", align_bytes=64)
-        val_word_pool = sb.tile([P, TOKENS], U32, name="val_word_pool", align_bytes=64)
+        val_word_pool = sb.tile([P, TOKENS], U32, name="val_word_pool", tag="val_word_pool", align_bytes=64)
         query_raw = sb.tile([P, PACK, ROWS], F32, name="query_raw")
         gout_raw = sb.tile([P, PACK, ROWS], F32, name="gout_raw")
         base_sb = sb.tile([P, SLOTS], F32, name="base_sb")
@@ -57,22 +57,22 @@ def tile_attend_gpdirect_smoothpage_kernel(
                 in_=scales[0, r:16:4, :].bitcast(I32),
             )
 
+        nc.gpsimd.dma_start(out=mix_sb[:], in_=mix)
         nc.sync.dma_start(offsets[:], offs)
-        for r in range(4):
-            load_scale_rows(nc.scalar, key_byte_pool, keys_scales, 0, r)
         nc.sync.dma_start(out=query_raw[:], in_=query.rearrange("(p j) q -> p j q", j=PACK))
-        nc.sync.dma_start(out=gout_raw[:], in_=gout.rearrange("(p j) q -> p j q", j=PACK))
         for r in range(4):
-            load_scale_rows(nc.scalar if r < 2 else nc.gpsimd, val_byte_pool, vals_scales, VALS_PLANE, r)
+            load_scale_rows(nc.sync, key_byte_pool, keys_scales, 0, r)
         nc.sync.dma_start(
             out=key_word_pool[:].bitcast(I32),
             in_=keys_words[0].rearrange("p n t -> p (n t)").bitcast(I32),
         )
+        nc.sync.dma_start(out=gout_raw[:], in_=gout.rearrange("(p j) q -> p j q", j=PACK))
+        for r in range(4):
+            load_scale_rows(nc.sync, val_byte_pool, vals_scales, VALS_PLANE, r)
         nc.sync.dma_start(
             out=val_word_pool[:].bitcast(I32),
             in_=vals_words[0].rearrange("p n t -> p (n t)").bitcast(I32),
         )
-        nc.gpsimd.dma_start(out=mix_sb[:], in_=mix)
         nc.sync.dma_start(out=base_sb[:], in_=base)
 
         keep = sb.tile([P, 1], F32, name="keep")
@@ -83,37 +83,56 @@ def tile_attend_gpdirect_smoothpage_kernel(
         key_bytes = sb.tile([P, SLOTS], U8, name="key_bytes", align_bytes=64)
         val_bytes = sb.tile([P, SLOTS], U8, name="val_bytes", align_bytes=64)
         nc.vector.tensor_copy(key_bytes[:], key_byte_pool[:].indirect(offsets[:]))
-        nc.vector.tensor_copy(val_bytes[:], val_byte_pool[:].indirect(offsets[:]))
 
-        grouped = sb.tile([P, 2, ROWS, PACK], BF16, name="grouped", align_bytes=64)
-        nc.scalar.copy(out=grouped[:, 0], in_=query_raw[:].rearrange("p j q -> p q j"))
-        nc.scalar.copy(out=grouped[:, 1], in_=gout_raw[:].rearrange("p j q -> p q j"))
-        row_codes = sb.tile([P, 2 * ROWS], U32, name="row_codes", align_bytes=64)
-        row_scales = sb.tile([P, 2 * ROWS], U8, name="row_scales", align_bytes=64)
-        nc.vector.quantize_mx(
-            out=row_codes[:].bitcast(FP8X4),
-            scales=row_scales[:],
-            in_=grouped[:].rearrange("p s q j -> p (s q j)"),
-        )
+        def quantize_rows(raw, name):
+            grouped = sb.tile([P, ROWS, PACK], BF16, name=name + "_grouped", align_bytes=64)
+            codes = sb.tile([P, ROWS], U32, name=name + "_codes", align_bytes=64)
+            scales = sb.tile([P, ROWS], U8, name=name + "_scales", align_bytes=64)
+            nc.scalar.copy(out=grouped[:], in_=raw[:].rearrange("p j q -> p q j"))
+            nc.vector.quantize_mx(
+                out=codes[:].bitcast(FP8X4), scales=scales[:], in_=grouped[:].rearrange("p q j -> p (q j)")
+            )
+            return codes, scales
+
+        query_codes, query_scales = quantize_rows(query_raw, "query")
 
         key_words = sb.tile([P, SLOTS], U32, name="key_words", align_bytes=64)
         nc.vector.tensor_copy(key_words[:], key_word_pool[:].indirect(offsets[:]))
         scores = psum.tile([P, SLOTS], F32, name="scores")
         nc.tensor.matmul_mx(
             out=scores[:],
-            lhsT=row_codes[:, 0:ROWS].bitcast(FP8X4),
-            lhsT_scale=row_scales[:, 0:ROWS],
+            lhsT=query_codes[:].bitcast(FP8X4),
+            lhsT_scale=query_scales[:],
             rhs=key_words[:].bitcast(FP8X4),
             rhs_scale=key_bytes[:],
             start=True,
             stop=True,
         )
 
-        neg_max = sb.tile([P, 1], F32, name="neg_max")
+        nc.vector.tensor_copy(val_bytes[:], val_byte_pool[:].indirect(offsets[:]))
+        gout_codes, gout_scales = quantize_rows(gout_raw, "gout")
+
+        val_words = [sb.tile([P, HALF], U32, name="val_words%d" % h, align_bytes=64) for h in range(2)]
+        c0 = [psum.tile([P, HALF], F32, name="c0_%d" % h) for h in range(2)]
+        for h in range(2):
+            list_cols = slice(h * HALF // 16, (h + 1) * HALF // 16)
+            nc.vector.tensor_copy(val_words[h][:], val_word_pool[:].indirect(offsets[:, list_cols]))
+            nc.tensor.matmul_mx(
+                out=c0[h][:],
+                lhsT=gout_codes[:].bitcast(FP8X4),
+                lhsT_scale=gout_scales[:],
+                rhs=val_words[h][:].bitcast(FP8X4),
+                rhs_scale=val_bytes[VALS_PLANE:P, halves[h]],
+                start=True,
+                stop=True,
+            )
+
+        neg_max = sb.tile([P, 1], F32, name="neg_max", tag="val_word_pool", align_bytes=64)
         nc.vector.tensor_reduce(neg_max[:], scores[:], AXIS_X, ALU.max, negate=True)
         p = sb.tile([P, SLOTS], F32, name="p")
         p_sum = sb.tile([P, 1], F32, name="p_sum")
         nc.scalar.activation(p[:], scores[:], ACT.Exp, bias=neg_max[:], scale=1.0, accum_out=p_sum[:])
+
         inv_sum = sb.tile([P, 1], F32, name="inv_sum")
         nc.vector.reciprocal(inv_sum[:], p_sum[:])
         r_sq = sb.tile([P, SLOTS], F32, name="r_sq")
@@ -123,21 +142,6 @@ def tile_attend_gpdirect_smoothpage_kernel(
         nc.scalar.activation(r[:], p[:], ACT.Copy, scale=inv_sum[:])
         r_sq_half = sb.tile([P, 1], F32, name="r_sq_half")
         nc.scalar.activation(r_sq_half[:], r_sq_sum[:], ACT.Copy, scale=ROOT_K / 2.0)
-
-        val_words = [sb.tile([P, HALF], U32, name="val_words%d" % h, align_bytes=64) for h in range(2)]
-        c0 = [psum.tile([P, HALF], F32, name="c0_%d" % h) for h in range(2)]
-        for h in range(2):
-            list_cols = slice(h * HALF // 16, (h + 1) * HALF // 16)
-            nc.vector.tensor_copy(val_words[h][:], val_word_pool[:].indirect(offsets[:, list_cols]))
-            nc.tensor.matmul_mx(
-                out=c0[h][:],
-                lhsT=row_codes[:, ROWS : 2 * ROWS].bitcast(FP8X4),
-                lhsT_scale=row_scales[:, ROWS : 2 * ROWS],
-                rhs=val_words[h][:].bitcast(FP8X4),
-                rhs_scale=val_bytes[VALS_PLANE:P, halves[h]],
-                start=True,
-                stop=True,
-            )
 
         runs = HALF // RUN
         run_sum = [sb.tile([P, runs], F32, name="run_sum%d" % h) for h in range(2)]

@@ -57,7 +57,6 @@ def tile_attend_gpdirect_smoothpage_kernel(
                 in_=scales[0, r:16:4, :].bitcast(I32),
             )
 
-        nc.gpsimd.dma_start(out=mix_sb[:], in_=mix)
         nc.sync.dma_start(offsets[:], offs)
         nc.sync.dma_start(out=query_raw[:], in_=query.rearrange("(p j) q -> p j q", j=PACK))
         for r in range(4):
@@ -66,19 +65,15 @@ def tile_attend_gpdirect_smoothpage_kernel(
             out=key_word_pool[:].bitcast(I32),
             in_=keys_words[0].rearrange("p n t -> p (n t)").bitcast(I32),
         )
-        nc.sync.dma_start(out=gout_raw[:], in_=gout.rearrange("(p j) q -> p j q", j=PACK))
         for r in range(4):
             load_scale_rows(nc.sync, val_byte_pool, vals_scales, VALS_PLANE, r)
+        nc.sync.dma_start(out=gout_raw[:], in_=gout.rearrange("(p j) q -> p j q", j=PACK))
         nc.sync.dma_start(
             out=val_word_pool[:].bitcast(I32),
             in_=vals_words[0].rearrange("p n t -> p (n t)").bitcast(I32),
         )
+        nc.sync.dma_start(out=mix_sb[:], in_=mix)
         nc.sync.dma_start(out=base_sb[:], in_=base)
-
-        keep = sb.tile([P, 1], F32, name="keep")
-        share = sb.tile([P, 1], F32, name="share")
-        nc.gpsimd.tensor_scalar(keep[:], mix_sb[:], -1.0, 1.0, ALU.mult, ALU.add)
-        nc.gpsimd.tensor_scalar(share[:], mix_sb[:], 1.0 / RUN, 0.0, ALU.mult, ALU.add)
 
         key_bytes = sb.tile([P, SLOTS], U8, name="key_bytes", align_bytes=64)
         val_bytes = sb.tile([P, SLOTS], U8, name="val_bytes", align_bytes=64)
@@ -111,6 +106,11 @@ def tile_attend_gpdirect_smoothpage_kernel(
 
         nc.vector.tensor_copy(val_bytes[:], val_byte_pool[:].indirect(offsets[:]))
         gout_codes, gout_scales = quantize_rows(gout_raw, "gout")
+
+        keep = sb.tile([P, 1], F32, name="keep")
+        share = sb.tile([P, 1], F32, name="share")
+        nc.scalar.activation(keep[:], mix_sb[:], ACT.Copy, bias=1.0, scale=-1.0)
+        nc.scalar.activation(share[:], mix_sb[:], ACT.Copy, scale=1.0 / RUN)
 
         val_words = [sb.tile([P, HALF], U32, name="val_words%d" % h, align_bytes=64) for h in range(2)]
         c0 = [psum.tile([P, HALF], F32, name="c0_%d" % h) for h in range(2)]

@@ -15,17 +15,20 @@ ACT = mybir.ActivationFunctionType
 AXIS_X = mybir.AxisListType.X
 
 P = 128
+QUADRANT = 32
 PACK = 4
+BLOCKS = 16
+BLOCKS_PER_QUADRANT = 4
+FEATURES = 512
 TOKENS = 2048
 SLOTS = 512
 ROWS = 128
 RUN = 8
 HALF = SLOTS // 2
-QUADRANT = 32
-VALS_PLANE = 4
+VALS_FIRST = 4
 ROOT_K = math.sqrt(512.0 * 2.0 * 512.0)
 
-FLOPS = 2 * 2 * 512 * ROWS * SLOTS
+FLOPS = 2 * 2 * FEATURES * ROWS * SLOTS
 
 
 def tile_attend_gpdirect_smoothpage_kernel(
@@ -38,49 +41,57 @@ def tile_attend_gpdirect_smoothpage_kernel(
         sb = ctx.enter_context(tc.tile_pool(name="sb", bufs=1))
         psum = ctx.enter_context(tc.psum_pool(name="psum", bufs=1))
 
+        def column(name):
+            return sb.tile([P, 1], F32, name=name)
+
+        def slot_tile(name):
+            return sb.tile([P, SLOTS], F32, name=name)
+
         offsets = sb.tile([P, SLOTS // 16], U16, name="offsets")
         key_byte_pool = sb.tile([P, TOKENS], U8, name="key_byte_pool", align_bytes=64)
-        val_byte_pool = sb.tile([P, TOKENS], U8, name="val_byte_pool", tag="val_byte_pool", align_bytes=64)
+        val_byte_pool = sb.tile([P, TOKENS], U8, name="val_byte_pool", align_bytes=64)
         key_word_pool = sb.tile([P, TOKENS], U32, name="key_word_pool", align_bytes=64)
-        val_word_pool = sb.tile([P, TOKENS], U32, name="val_word_pool", tag="val_word_pool", align_bytes=64)
+        val_word_pool = sb.tile([P, TOKENS], U32, name="val_word_pool", align_bytes=64)
         query_raw = sb.tile([P, PACK, ROWS], F32, name="query_raw")
         gout_raw = sb.tile([P, PACK, ROWS], F32, name="gout_raw")
-        base_sb = sb.tile([P, SLOTS], F32, name="base_sb")
-        mix_sb = sb.tile([P, 1], F32, name="mix_sb")
+        base_sb = slot_tile("base_sb")
+        mix_sb = column("mix_sb")
 
         nc.vector.memset(key_byte_pool[:].bitcast(I32), 0)
         nc.vector.memset(val_byte_pool[:].bitcast(I32), 0)
 
-        def load_scale_rows(queue, byte_pool, scales, plane, r):
-            queue.dma_start(
-                out=byte_pool[plane + r : P : QUADRANT, :].bitcast(I32),
-                in_=scales[0, r:16:4, :].bitcast(I32),
+        def load_rows(raw, rows):
+            nc.sync.dma_start(out=raw[:], in_=rows.rearrange("(p j) q -> p j q", j=PACK))
+
+        def load_words(word_pool, words):
+            nc.sync.dma_start(
+                out=word_pool[:].bitcast(I32), in_=words[0].rearrange("p n t -> p (n t)").bitcast(I32)
             )
 
+        def load_scale_bytes(byte_pool, scales, first):
+            for place in range(BLOCKS_PER_QUADRANT):
+                nc.sync.dma_start(
+                    out=byte_pool[first + place : P : QUADRANT, :].bitcast(I32),
+                    in_=scales[0, place:BLOCKS:BLOCKS_PER_QUADRANT, :].bitcast(I32),
+                )
+
         nc.sync.dma_start(offsets[:], offs)
-        nc.sync.dma_start(out=query_raw[:], in_=query.rearrange("(p j) q -> p j q", j=PACK))
-        for r in range(4):
-            load_scale_rows(nc.sync, key_byte_pool, keys_scales, 0, r)
-        nc.sync.dma_start(
-            out=key_word_pool[:].bitcast(I32),
-            in_=keys_words[0].rearrange("p n t -> p (n t)").bitcast(I32),
-        )
-        for r in range(4):
-            load_scale_rows(nc.sync, val_byte_pool, vals_scales, VALS_PLANE, r)
-        nc.sync.dma_start(out=gout_raw[:], in_=gout.rearrange("(p j) q -> p j q", j=PACK))
-        nc.sync.dma_start(
-            out=val_word_pool[:].bitcast(I32),
-            in_=vals_words[0].rearrange("p n t -> p (n t)").bitcast(I32),
-        )
+        load_rows(query_raw, query)
+        load_scale_bytes(key_byte_pool, keys_scales, 0)
+        load_words(key_word_pool, keys_words)
+        load_scale_bytes(val_byte_pool, vals_scales, VALS_FIRST)
+        load_words(val_word_pool, vals_words)
+        load_rows(gout_raw, gout)
         nc.sync.dma_start(out=mix_sb[:], in_=mix)
         nc.sync.dma_start(out=base_sb[:], in_=base)
 
-        key_bytes = sb.tile([P, SLOTS], U8, name="key_bytes", align_bytes=64)
-        val_bytes = sb.tile([P, SLOTS], U8, name="val_bytes", align_bytes=64)
-        nc.vector.tensor_copy(key_bytes[:], key_byte_pool[:].indirect(offsets[:]))
+        def gather(pool_tile, dtype, name):
+            picked = sb.tile([P, SLOTS], dtype, name=name, align_bytes=64)
+            nc.vector.tensor_copy(picked[:], pool_tile[:].indirect(offsets[:]))
+            return picked
 
         def quantize_rows(raw, name):
-            grouped = sb.tile([P, ROWS, PACK], BF16, name=name + "_grouped", align_bytes=64)
+            grouped = sb.tile([P, ROWS, PACK], BF16, name=name + "_grouped", tag=name + "_grouped", align_bytes=64)
             codes = sb.tile([P, ROWS], U32, name=name + "_codes", align_bytes=64)
             scales = sb.tile([P, ROWS], U8, name=name + "_scales", align_bytes=64)
             nc.scalar.copy(out=grouped[:], in_=raw[:].rearrange("p j q -> p q j"))
@@ -89,10 +100,9 @@ def tile_attend_gpdirect_smoothpage_kernel(
             )
             return codes, scales
 
+        key_bytes = gather(key_byte_pool, U8, "key_bytes")
         query_codes, query_scales = quantize_rows(query_raw, "query")
-
-        key_words = sb.tile([P, SLOTS], U32, name="key_words", align_bytes=64)
-        nc.vector.tensor_copy(key_words[:], key_word_pool[:].indirect(offsets[:]))
+        key_words = gather(key_word_pool, U32, "key_words")
         scores = psum.tile([P, SLOTS], F32, name="scores")
         nc.tensor.matmul_mx(
             out=scores[:],
@@ -104,103 +114,84 @@ def tile_attend_gpdirect_smoothpage_kernel(
             stop=True,
         )
 
-        nc.vector.tensor_copy(val_bytes[:], val_byte_pool[:].indirect(offsets[:]))
+        val_bytes = gather(val_byte_pool, U8, "val_bytes")
+        val_words = gather(val_word_pool, U32, "val_words")
         gout_codes, gout_scales = quantize_rows(gout_raw, "gout")
-
-        keep = sb.tile([P, 1], F32, name="keep")
-        share = sb.tile([P, 1], F32, name="share")
-        nc.scalar.activation(keep[:], mix_sb[:], ACT.Copy, bias=1.0, scale=-1.0)
-        nc.scalar.activation(share[:], mix_sb[:], ACT.Copy, scale=1.0 / RUN)
-
-        val_words = [sb.tile([P, HALF], U32, name="val_words%d" % h, align_bytes=64) for h in range(2)]
         c0 = [psum.tile([P, HALF], F32, name="c0_%d" % h) for h in range(2)]
         for h in range(2):
-            list_cols = slice(h * HALF // 16, (h + 1) * HALF // 16)
-            nc.vector.tensor_copy(val_words[h][:], val_word_pool[:].indirect(offsets[:, list_cols]))
             nc.tensor.matmul_mx(
                 out=c0[h][:],
                 lhsT=gout_codes[:].bitcast(FP8X4),
                 lhsT_scale=gout_scales[:],
-                rhs=val_words[h][:].bitcast(FP8X4),
-                rhs_scale=val_bytes[VALS_PLANE:P, halves[h]],
+                rhs=val_words[:, halves[h]].bitcast(FP8X4),
+                rhs_scale=val_bytes[VALS_FIRST:P, halves[h]],
                 start=True,
                 stop=True,
             )
 
-        neg_max = sb.tile([P, 1], F32, name="neg_max", tag="val_word_pool", align_bytes=64)
-        nc.vector.tensor_reduce(neg_max[:], scores[:], AXIS_X, ALU.max, negate=True)
-        p = sb.tile([P, SLOTS], F32, name="p")
-        p_sum = sb.tile([P, 1], F32, name="p_sum")
-        nc.scalar.activation(p[:], scores[:], ACT.Exp, bias=neg_max[:], scale=1.0, accum_out=p_sum[:])
+        keep = column("keep")
+        share = column("share")
+        nc.scalar.activation(keep[:], mix_sb[:], ACT.Copy, bias=1.0, scale=-1.0)
+        nc.scalar.activation(share[:], mix_sb[:], ACT.Copy, scale=1.0 / RUN)
 
-        inv_sum = sb.tile([P, 1], F32, name="inv_sum")
+        neg_max = sb.tile([P, 1], F32, name="neg_max", tag="gout_grouped", align_bytes=64)
+        nc.vector.tensor_reduce(neg_max[:], scores[:], AXIS_X, ALU.max, negate=True)
+        p = slot_tile("p")
+        p_sum = column("p_sum")
+        nc.scalar.activation(p[:], scores[:], ACT.Exp, bias=neg_max[:], scale=1.0, accum_out=p_sum[:])
+        inv_sum = column("inv_sum")
         nc.vector.reciprocal(inv_sum[:], p_sum[:])
-        r_sq = sb.tile([P, SLOTS], F32, name="r_sq")
-        r_sq_sum = sb.tile([P, 1], F32, name="r_sq_sum")
+        r_sq = slot_tile("r_sq")
+        r_sq_sum = column("r_sq_sum")
         nc.scalar.activation(r_sq[:], p[:], ACT.Square, scale=inv_sum[:], accum_out=r_sq_sum[:])
-        r = sb.tile([P, SLOTS], F32, name="r")
+        r = slot_tile("r")
         nc.scalar.activation(r[:], p[:], ACT.Copy, scale=inv_sum[:])
-        r_sq_half = sb.tile([P, 1], F32, name="r_sq_half")
-        nc.scalar.activation(r_sq_half[:], r_sq_sum[:], ACT.Copy, scale=ROOT_K / 2.0)
+        r_sq_scaled = column("r_sq_scaled")
+        nc.scalar.activation(r_sq_scaled[:], r_sq_sum[:], ACT.Copy, scale=ROOT_K / 2.0)
 
         runs = HALF // RUN
         run_sum = [sb.tile([P, runs], F32, name="run_sum%d" % h) for h in range(2)]
-        run_mix = [sb.tile([P, runs], F32, name="run_mix%d" % h) for h in range(2)]
-        dr = sb.tile([P, SLOTS], F32, name="dr")
+        run_term = [sb.tile([P, runs], F32, name="run_term%d" % h) for h in range(2)]
+        dr = slot_tile("dr")
         for h in range(2):
             nc.vector.tensor_reduce(
                 run_sum[h][:], c0[h][:].rearrange("p (g j) -> p g j", j=RUN), AXIS_X, ALU.add
             )
         for h in range(2):
-            nc.vector.tensor_scalar(run_mix[h][:], run_sum[h][:], share[:], None, ALU.mult)
+            nc.vector.tensor_scalar(run_term[h][:], run_sum[h][:], share[:], None, ALU.mult)
         for h in range(2):
             nc.vector.scalar_tensor_tensor(
                 dr[:, halves[h]].rearrange("p (g j) -> p g j", j=RUN),
                 c0[h][:].rearrange("p (g j) -> p g j", j=RUN),
                 keep[:],
-                run_mix[h][:].unsqueeze(2).to_broadcast([P, runs, RUN]),
+                run_term[h][:].unsqueeze(2).to_broadcast([P, runs, RUN]),
                 ALU.mult,
                 ALU.add,
             )
 
-        terms = sb.tile([P, SLOTS], F32, name="terms")
-        terms2 = sb.tile([P, SLOTS], F32, name="terms2")
-        mu = sb.tile([P, 1], F32, name="mu")
-        nc.vector.scalar_tensor_tensor(terms[:], dr[:], inv_sum[:], p[:], ALU.mult, ALU.mult, accum_out=mu[:])
-        raw_t1 = sb.tile([P, 1], F32, name="raw_t1")
+        mu_terms = slot_tile("mu_terms")
+        mu = column("mu")
+        nc.vector.scalar_tensor_tensor(mu_terms[:], dr[:], inv_sum[:], p[:], ALU.mult, ALU.mult, accum_out=mu[:])
+        dr_r_sq_terms = slot_tile("dr_r_sq_terms")
+        dr_r_sq = column("dr_r_sq")
         nc.vector.scalar_tensor_tensor(
-            terms2[:], dr[:], ROOT_K / 2.0, r_sq[:], ALU.mult, ALU.mult, accum_out=raw_t1[:]
+            dr_r_sq_terms[:], dr[:], ROOT_K / 2.0, r_sq[:], ALU.mult, ALU.mult, accum_out=dr_r_sq[:]
         )
 
-        da = sb.tile([P, SLOTS], F32, name="da")
-        shift = sb.tile([P, 1], F32, name="shift")
-        shift_sq = sb.tile([P, 1], F32, name="shift_sq")
-        shift_sq_all = sb.tile([P, 1], F32, name="shift_sq_all")
-        square = sb.tile([P, SLOTS], F32, name="square")
-        square_sum = [sb.tile([P, 1], F32, name="square_sum%d" % h) for h in range(2)]
+        da = slot_tile("da")
+        square = slot_tile("square")
+        partial = slot_tile("partial")
+        result = slot_tile("result")
+        shift = column("shift")
+        shift_sq = column("shift_sq")
+        shift_sq_row = column("shift_sq_row")
+        square_sum = [column("square_sum%d" % h) for h in range(2)]
+        neg_k_t2 = column("neg_k_t2")
 
         def make_da(h):
             nc.vector.scalar_tensor_tensor(
                 da[:, halves[h]], dr[:, halves[h]], mu[:], r[:, halves[h]], ALU.subtract, ALU.mult
             )
-
-        def make_square(h):
-            nc.scalar.activation(
-                square[:, halves[h]], da[:, halves[h]], ACT.Square,
-                bias=shift[:], scale=ROOT_K, accum_out=square_sum[h][:],
-            )
-
-        make_da(0)
-        nc.vector.scalar_tensor_tensor(shift[:], mu[:], r_sq_half[:], raw_t1[:], ALU.mult, ALU.subtract)
-        make_da(1)
-        make_square(0)
-        make_square(1)
-        nc.vector.tensor_tensor(shift_sq[:], shift[:], shift[:], ALU.mult)
-        nc.vector.scalar_tensor_tensor(shift_sq_all[:], shift[:], float(SLOTS), shift[:], ALU.mult, ALU.mult)
-
-        partial = sb.tile([P, SLOTS], F32, name="partial")
-        result = sb.tile([P, SLOTS], F32, name="result")
-        neg_t2 = sb.tile([P, 1], F32, name="neg_t2")
 
         def make_partial(h):
             nc.vector.scalar_tensor_tensor(
@@ -208,13 +199,24 @@ def tile_attend_gpdirect_smoothpage_kernel(
                 ALU.subtract, ALU.add,
             )
 
+        make_da(0)
+        nc.vector.scalar_tensor_tensor(shift[:], mu[:], r_sq_scaled[:], dr_r_sq[:], ALU.mult, ALU.subtract)
+        make_da(1)
+        for h in range(2):
+            nc.scalar.activation(
+                square[:, halves[h]], da[:, halves[h]], ACT.Square,
+                bias=shift[:], scale=ROOT_K, accum_out=square_sum[h][:],
+            )
+        nc.vector.tensor_tensor(shift_sq[:], shift[:], shift[:], ALU.mult)
+        nc.vector.scalar_tensor_tensor(shift_sq_row[:], shift[:], float(SLOTS), shift[:], ALU.mult, ALU.mult)
+
         make_partial(0)
         nc.vector.tensor_scalar(
-            neg_t2[:], shift_sq_all[:], square_sum[0][:], square_sum[1][:], ALU.subtract, ALU.subtract
+            neg_k_t2[:], shift_sq_row[:], square_sum[0][:], square_sum[1][:], ALU.subtract, ALU.subtract
         )
         make_partial(1)
         for h in range(2):
             nc.vector.scalar_tensor_tensor(
-                result[:, halves[h]], r[:, halves[h]], neg_t2[:], partial[:, halves[h]], ALU.mult, ALU.add
+                result[:, halves[h]], r[:, halves[h]], neg_k_t2[:], partial[:, halves[h]], ALU.mult, ALU.add
             )
             nc.sync.dma_start(out=out[:, halves[h]], in_=result[:, halves[h]])

@@ -25,6 +25,7 @@ SLOTS = 512
 ROWS = 128
 RUN = 8
 HALF = SLOTS // 2
+LINE = 4
 VALS_FIRST = 4
 ROOT_K = math.sqrt(512.0 * 2.0 * 512.0)
 
@@ -94,7 +95,10 @@ def tile_attend_gpdirect_smoothpage_kernel(
             grouped = sb.tile([P, ROWS, PACK], BF16, name=name + "_grouped", tag=name + "_grouped", align_bytes=64)
             codes = sb.tile([P, ROWS], U32, name=name + "_codes", align_bytes=64)
             scales = sb.tile([P, ROWS], U8, name=name + "_scales", align_bytes=64)
-            nc.scalar.copy(out=grouped[:], in_=raw[:].rearrange("p j q -> p q j"))
+            nc.scalar.copy(
+                out=grouped[:].rearrange("p (c n) j -> p c j n", n=LINE),
+                in_=raw[:].rearrange("p j (c n) -> p c j n", n=LINE),
+            )
             nc.vector.quantize_mx(
                 out=codes[:].bitcast(FP8X4), scales=scales[:], in_=grouped[:].rearrange("p q j -> p (q j)")
             )

import math
from contextlib import ExitStack

import concourse.mybir as mybir

F32 = mybir.dt.float32
BF16 = mybir.dt.bfloat16
I32 = mybir.dt.int32
U32 = mybir.dt.uint32
U16 = mybir.dt.uint16
U8 = mybir.dt.uint8
FP8X4 = mybir.dt.float8_e4m3fn_x4
ALU = mybir.AluOpType
ACT = mybir.ActivationFunctionType
AXIS_X = mybir.AxisListType.X

P = 128
QUADRANT = 32
PACK = 4
BLOCKS = 16
BLOCKS_PER_QUADRANT = 4
FEATURES = 512
TOKENS = 2048
SLOTS = 512
ROWS = 128
RUN = 8
HALF = SLOTS // 2
LINE = 4
VALS_FIRST = 4
ROOT_K = math.sqrt(512.0 * 2.0 * 512.0)

FLOPS = 2 * 2 * FEATURES * ROWS * SLOTS


def tile_attend_gpdirect_smoothpage_kernel(
    tc, query, keys_words, keys_scales, mix, gout, vals_words, vals_scales, base, offs, out
):
    nc = tc.nc
    halves = [slice(0, HALF), slice(HALF, SLOTS)]

    with ExitStack() as ctx:
        sb = ctx.enter_context(tc.tile_pool(name="sb", bufs=1))
        psum = ctx.enter_context(tc.psum_pool(name="psum", bufs=1))

        def column(name):
            return sb.tile([P, 1], F32, name=name)

        def slot_tile(name):
            return sb.tile([P, SLOTS], F32, name=name)

        offsets = sb.tile([P, SLOTS // 16], U16, name="offsets")
        key_byte_pool = sb.tile([P, TOKENS], U8, name="key_byte_pool", align_bytes=64)
        val_byte_pool = sb.tile([P, TOKENS], U8, name="val_byte_pool", align_bytes=64)
        key_word_pool = sb.tile([P, TOKENS], U32, name="key_word_pool", align_bytes=64)
        val_word_pool = sb.tile([P, TOKENS], U32, name="val_word_pool", align_bytes=64)
        query_raw = sb.tile([P, PACK, ROWS], F32, name="query_raw")
        gout_raw = sb.tile([P, PACK, ROWS], F32, name="gout_raw")
        base_sb = slot_tile("base_sb")
        mix_sb = column("mix_sb")

        nc.vector.memset(key_byte_pool[:].bitcast(I32), 0)
        nc.vector.memset(val_byte_pool[:].bitcast(I32), 0)

        def load_rows(raw, rows):
            nc.sync.dma_start(out=raw[:], in_=rows.rearrange("(p j) q -> p j q", j=PACK))

        def load_words(word_pool, words):
            nc.sync.dma_start(
                out=word_pool[:].bitcast(I32), in_=words[0].rearrange("p n t -> p (n t)").bitcast(I32)
            )

        def load_scale_bytes(byte_pool, scales, first):
            for place in range(BLOCKS_PER_QUADRANT):
                nc.sync.dma_start(
                    out=byte_pool[first + place : P : QUADRANT, :].bitcast(I32),
                    in_=scales[0, place:BLOCKS:BLOCKS_PER_QUADRANT, :].bitcast(I32),
                )

        nc.sync.dma_start(offsets[:], offs)
        load_rows(query_raw, query)
        load_scale_bytes(key_byte_pool, keys_scales, 0)
        load_words(key_word_pool, keys_words)
        load_scale_bytes(val_byte_pool, vals_scales, VALS_FIRST)
        load_words(val_word_pool, vals_words)
        load_rows(gout_raw, gout)
        nc.sync.dma_start(out=mix_sb[:], in_=mix)
        nc.sync.dma_start(out=base_sb[:], in_=base)

        def gather(pool_tile, dtype, name):
            picked = sb.tile([P, SLOTS], dtype, name=name, align_bytes=64)
            nc.vector.tensor_copy(picked[:], pool_tile[:].indirect(offsets[:]))
            return picked

        def quantize_rows(raw, name):
            grouped = sb.tile([P, ROWS, PACK], BF16, name=name + "_grouped", tag=name + "_grouped", align_bytes=64)
            codes = sb.tile([P, ROWS], U32, name=name + "_codes", align_bytes=64)
            scales = sb.tile([P, ROWS], U8, name=name + "_scales", align_bytes=64)
            nc.scalar.copy(
                out=grouped[:].rearrange("p (c n) j -> p c j n", n=LINE),
                in_=raw[:].rearrange("p j (c n) -> p c j n", n=LINE),
            )
            nc.vector.quantize_mx(
                out=codes[:].bitcast(FP8X4), scales=scales[:], in_=grouped[:].rearrange("p q j -> p (q j)")
            )
            return codes, scales

        key_bytes = gather(key_byte_pool, U8, "key_bytes")
        query_codes, query_scales = quantize_rows(query_raw, "query")
        key_words = gather(key_word_pool, U32, "key_words")
        scores = psum.tile([P, SLOTS], F32, name="scores")
        nc.tensor.matmul_mx(
            out=scores[:],
            lhsT=query_codes[:].bitcast(FP8X4),
            lhsT_scale=query_scales[:],
            rhs=key_words[:].bitcast(FP8X4),
            rhs_scale=key_bytes[:],
            start=True,
            stop=True,
        )

        val_bytes = gather(val_byte_pool, U8, "val_bytes")
        val_words = gather(val_word_pool, U32, "val_words")
        gout_codes, gout_scales = quantize_rows(gout_raw, "gout")
        c0 = [psum.tile([P, HALF], F32, name="c0_%d" % h) for h in range(2)]
        for h in range(2):
            nc.tensor.matmul_mx(
                out=c0[h][:],
                lhsT=gout_codes[:].bitcast(FP8X4),
                lhsT_scale=gout_scales[:],
                rhs=val_words[:, halves[h]].bitcast(FP8X4),
                rhs_scale=val_bytes[VALS_FIRST:P, halves[h]],
                start=True,
                stop=True,
            )

        keep = column("keep")
        share = column("share")
        nc.scalar.activation(keep[:], mix_sb[:], ACT.Copy, bias=1.0, scale=-1.0)
        nc.scalar.activation(share[:], mix_sb[:], ACT.Copy, scale=1.0 / RUN)

        neg_max = sb.tile([P, 1], F32, name="neg_max", tag="gout_grouped", align_bytes=64)
        nc.vector.tensor_reduce(neg_max[:], scores[:], AXIS_X, ALU.max, negate=True)
        p = slot_tile("p")
        p_sum = column("p_sum")
        nc.scalar.activation(p[:], scores[:], ACT.Exp, bias=neg_max[:], scale=1.0, accum_out=p_sum[:])
        inv_sum = column("inv_sum")
        nc.vector.reciprocal(inv_sum[:], p_sum[:])
        r_sq = slot_tile("r_sq")
        r_sq_sum = column("r_sq_sum")
        nc.scalar.activation(r_sq[:], p[:], ACT.Square, scale=inv_sum[:], accum_out=r_sq_sum[:])
        r = slot_tile("r")
        nc.scalar.activation(r[:], p[:], ACT.Copy, scale=inv_sum[:])
        r_sq_scaled = column("r_sq_scaled")
        nc.scalar.activation(r_sq_scaled[:], r_sq_sum[:], ACT.Copy, scale=ROOT_K / 2.0)

        runs = HALF // RUN
        run_sum = [sb.tile([P, runs], F32, name="run_sum%d" % h) for h in range(2)]
        run_term = [sb.tile([P, runs], F32, name="run_term%d" % h) for h in range(2)]
        dr = slot_tile("dr")
        for h in range(2):
            nc.vector.tensor_reduce(
                run_sum[h][:], c0[h][:].rearrange("p (g j) -> p g j", j=RUN), AXIS_X, ALU.add
            )
        for h in range(2):
            nc.vector.tensor_scalar(run_term[h][:], run_sum[h][:], share[:], None, ALU.mult)
        for h in range(2):
            nc.vector.scalar_tensor_tensor(
                dr[:, halves[h]].rearrange("p (g j) -> p g j", j=RUN),
                c0[h][:].rearrange("p (g j) -> p g j", j=RUN),
                keep[:],
                run_term[h][:].unsqueeze(2).to_broadcast([P, runs, RUN]),
                ALU.mult,
                ALU.add,
            )

        mu_terms = slot_tile("mu_terms")
        mu = column("mu")
        nc.vector.scalar_tensor_tensor(mu_terms[:], dr[:], inv_sum[:], p[:], ALU.mult, ALU.mult, accum_out=mu[:])
        dr_r_sq_terms = slot_tile("dr_r_sq_terms")
        dr_r_sq = column("dr_r_sq")
        nc.vector.scalar_tensor_tensor(
            dr_r_sq_terms[:], dr[:], ROOT_K / 2.0, r_sq[:], ALU.mult, ALU.mult, accum_out=dr_r_sq[:]
        )

        da = slot_tile("da")
        square = slot_tile("square")
        partial = slot_tile("partial")
        result = slot_tile("result")
        shift = column("shift")
        shift_sq = column("shift_sq")
        shift_sq_row = column("shift_sq_row")
        square_sum = [column("square_sum%d" % h) for h in range(2)]
        neg_k_t2 = column("neg_k_t2")

        def make_da(h):
            nc.vector.scalar_tensor_tensor(
                da[:, halves[h]], dr[:, halves[h]], mu[:], r[:, halves[h]], ALU.subtract, ALU.mult
            )

        def make_partial(h):
            nc.vector.scalar_tensor_tensor(
                partial[:, halves[h]], square[:, halves[h]], shift_sq[:], base_sb[:, halves[h]],
                ALU.subtract, ALU.add,
            )

        make_da(0)
        nc.vector.scalar_tensor_tensor(shift[:], mu[:], r_sq_scaled[:], dr_r_sq[:], ALU.mult, ALU.subtract)
        make_da(1)
        for h in range(2):
            nc.scalar.activation(
                square[:, halves[h]], da[:, halves[h]], ACT.Square,
                bias=shift[:], scale=ROOT_K, accum_out=square_sum[h][:],
            )
        nc.vector.tensor_tensor(shift_sq[:], shift[:], shift[:], ALU.mult)
        nc.vector.scalar_tensor_tensor(shift_sq_row[:], shift[:], float(SLOTS), shift[:], ALU.mult, ALU.mult)

        make_partial(0)
        nc.vector.tensor_scalar(
            neg_k_t2[:], shift_sq_row[:], square_sum[0][:], square_sum[1][:], ALU.subtract, ALU.subtract
        )
        make_partial(1)
        for h in range(2):
            nc.vector.scalar_tensor_tensor(
                result[:, halves[h]], r[:, halves[h]], neg_k_t2[:], partial[:, halves[h]], ALU.mult, ALU.add
            )
            nc.sync.dma_start(out=out[:, halves[h]], in_=result[:, halves[h]])
